import numpy as np
import ml_dtypes


def mxq(x, axis, fmt="e4m3"):
    dtype, down = {"e4m3": (ml_dtypes.float8_e4m3fn, 7), "e5m2": (ml_dtypes.float8_e5m2, 14)}[fmt]
    v = np.moveaxis(np.asarray(x, np.float32).astype(ml_dtypes.bfloat16).astype(np.float64), axis, -1)
    blocks = v.reshape(v.shape[:-1] + (-1, 32))
    amax = np.abs(blocks).max(-1, keepdims=True)
    byte = np.maximum(np.where(amax > 0, np.frexp(amax)[1] - 1 + 127, 0) - down, 1)
    scale = np.exp2(byte - 127.0)
    codes = (blocks / scale).astype(np.float32).astype(dtype).astype(np.float64)
    return np.moveaxis((codes * scale).reshape(v.shape), -1, axis)


WIDE = False


def mx_kscale(k):
    if not WIDE:
        return np.ones(k)
    levels = np.array([10, -10, 5, -5, 0])
    if k % 512:
        return np.exp2(np.random.permutation(np.resize(levels, k // 32))).repeat(32)
    a = np.empty((k // 512, 16))
    for p in range(k // 512):
        a[p, :8] = np.random.permutation(np.resize(levels, 8))
        for g in range(8):
            far = levels[np.abs(levels - a[p, g]) >= 10]
            a[p, g + 8] = far[np.random.randint(len(far))]
    return np.exp2(a.ravel()).repeat(32)


BF16 = ml_dtypes.bfloat16


def bf(x):
    return np.asarray(x, np.float32).astype(BF16)


def f64(x):
    return np.asarray(x).astype(np.float64)


E2M1 = np.array([0.0, 0.5, 1.0, 1.5, 2.0, 3.0, 4.0, 6.0, -0.0, -0.5, -1.0, -1.5, -2.0, -3.0, -4.0, -6.0])


def pack_weight(w, fmt):
    k, n = w.shape
    w = f64(bf(w)).reshape(k // 32, 32, n)
    amax = np.abs(w).max(1)
    if fmt == "e4m3":
        byte = np.frexp(amax)[1] - 1 + 127 - 7
    else:
        mant, ex = np.frexp(amax / 6.0)
        byte = np.where(mant > 0.5, ex, ex - 1) + 127
    byte = np.clip(np.where(amax > 0, byte, 1), 1, 254)
    scaled = (w * np.exp2(127.0 - byte)[:, None, :]).reshape(k, n).astype(np.float32)
    by_word = np.ascontiguousarray(scaled.reshape(k // 512, 128, 4, n).transpose(0, 1, 3, 2))
    if fmt == "e4m3":
        words = by_word.astype(ml_dtypes.float8_e4m3fn).view(np.uint8)
    else:
        c = by_word.astype(ml_dtypes.float4_e2m1fn).view(np.uint8) & 0xF
        words = c[..., 0::2] | (c[..., 1::2] << 4)
    return np.ascontiguousarray(words), np.ascontiguousarray(byte.astype(np.uint8).reshape(k // 512, 16, n))


def unpack_weight(words, scales, fmt):
    g, p, n, _ = words.shape
    if fmt == "e4m3":
        vals = np.ascontiguousarray(words).view(ml_dtypes.float8_e4m3fn).astype(np.float64)
    else:
        nib = np.empty((g, p, n, 4), np.uint8)
        nib[..., 0::2] = words & 0xF
        nib[..., 1::2] = words >> 4
        vals = E2M1[nib]
    vals = vals * np.repeat(np.exp2(scales.astype(np.float64) - 127.0), 8, axis=1)[..., None]
    return vals.transpose(0, 1, 3, 2).reshape(g * 512, n)
def pack4(w):
    words, scales = pack_weight(w, "e2m1")
    return words.reshape(words.shape[0], 128, -1), scales


def unpack4(words, scales):
    return unpack_weight(words.reshape(words.shape[0], 128, -1, 2), scales, "e2m1")


M, D, J, C = 1024, 1024, 1024, 1536


def setup_inputs():
    s = mx_kscale(D)
    r = mx_kscale(D)
    t = mx_kscale(J)
    x = np.random.standard_normal((D, J))
    frames = np.random.standard_normal((D, M)) / np.sqrt(D)
    frames_words, frames_scales = pack4(frames * s[:, None])
    refs_words, refs_scales = pack4(x / s[:, None])
    return {"frames_words": frames_words,
            "frames_scales": frames_scales,
            "refs_words": refs_words,
            "refs_scales": refs_scales,
            "coef": bf(np.random.standard_normal(J) * J ** -0.25 * t),
            "xref": bf(x.T * J ** -0.25 * r / t[:, None]),
            "jac": bf(np.random.standard_normal((D, C)) / np.sqrt(D) / r[:, None]),
            "base": bf(0.4 * np.random.standard_normal(C))}


def reference(frames_words, frames_scales, refs_words, refs_scales, coef, xref, jac, base):
    a = unpack4(frames_words, frames_scales)
    x = unpack4(refs_words, refs_scales)
    u = a.T @ x
    h = u ** 2 * f64(coef)
    v = mxq(f64(xref), 1, "e4m3") @ mxq(f64(jac), 0, "e4m3")
    force = mxq(h, 1, "e4m3") @ mxq(v, 0, "e4m3")
    return force + f64(base)

@@ -1,0 +1,324 @@
+from contextlib import ExitStack
+
+import concourse.mybir as mybir
+from concourse.masks import make_identity
+
+M, D, J, C = 1024, 1024, 1024, 1536
+FLOPS = 2 * M * D * J + 2 * J * D * C + 2 * M * J * C
+
+F32 = mybir.dt.float32
+BF16 = mybir.dt.bfloat16
+I32 = mybir.dt.int32
+U32 = mybir.dt.uint32
+U8 = mybir.dt.uint8
+FP8X4 = mybir.dt.float8_e4m3fn_x4
+FP4X4 = mybir.dt.float4_e2m1fn_x4
+SQUARE = mybir.ActivationFunctionType.Square
+MULT = mybir.AluOpType.mult
+ADD = mybir.AluOpType.add
+
+P = 128
+PACK = 4
+KP = 512
+BANK = 512
+MC = 256
+CC = 512
+
+
+def tile_cubic_kernel_forces_s12_kernel(
+    tc, frames_words, frames_scales, refs_words, refs_scales, coef, xref, jac, base, out
+):
+    nc = tc.nc
+    with ExitStack() as ctx:
+        keep = ctx.enter_context(tc.tile_pool(name="keep", bufs=1))
+        ring = ctx.enter_context(tc.tile_pool(name="ring", bufs=2))
+        psum = ctx.enter_context(tc.psum_pool(name="psum", bufs=8))
+        ctx.enter_context(tc.manual_schedule())
+
+        def kept(name, shape, dtype):
+            return keep.tile(shape, dtype, name=name, align_bytes=64)
+
+        def new_bank():
+            return psum.tile([P, BANK], F32, name="bank")
+
+        refs_raw = kept("refs_raw", [P, 2, 2 * J], U8)
+        refs_sc_raw = kept("refs_sc_raw", [P, 2, J], U8)
+        frames_sc = kept("frames_sc", [P, 2, M], U8)
+        frames = [kept("frames%d" % h, [P, 2, M], U8) for h in range(2)]
+        refs = [kept("refs%d" % jg, [P, 2, J], U8) for jg in range(2)]
+        refs_sc = [kept("refs_sc%d" % jg, [P, 2, KP], U8) for jg in range(2)]
+        coef_rows = kept("coef_rows", [PACK, 2 * P], BF16)
+        coef_wide = kept("coef_wide", [P, 2 * P], F32)
+        coef_slot = kept("coef_slot", [P, 2, PACK], F32)
+        ident = kept("ident", [P, P], F32)
+        base_rows = kept("base_rows", [P, C], BF16)
+        xref_raw = {(jg, h): kept("xref_raw%d%d" % (jg, h), [P, 2, D], BF16) for jg in range(2) for h in range(2)}
+        jac_raw = {(cc, g): kept("jac_raw%d%d" % (cc, g), [P, PACK, CC], BF16) for cc in range(3) for g in range(2)}
+
+        def mx_pair(name):
+            return kept(name + "_codes", [P, 512], U32), kept(name + "_scales", [P, 512], U8)
+
+        xref_q = {(jg, g): mx_pair("xref_q%d%d" % (jg, g)) for jg in range(2) for g in range(2)}
+        jac_q = {(cc, g): mx_pair("jac_q%d%d" % (cc, g)) for cc in range(3) for g in range(2)}
+        v_q = {(cc, jg): mx_pair("v_q%d%d" % (cc, jg)) for cc in range(3) for jg in range(2)}
+        h_q = [mx_pair("h_q%d" % mc) for mc in range(4)]
+
+        squares, h_bf, xref_bf, jac_bf, v_bf = {}, {}, {}, {}, {}
+
+        def quantize(pair, src):
+            codes, scales = pair
+            nc.vector.quantize_mx(out=codes[:].bitcast(FP8X4), scales=scales[:], in_=src)
+
+        def load_scale_rows(queue, plane, scales):
+            rows = scales.rearrange("g (a r) n -> r a g n", r=4)
+            for r in range(4):
+                queue.dma_start(out=plane[:].bitcast(I32)[r:P:32], in_=rows[r].bitcast(I32))
+
+        def load_frames(h):
+            nc.sync.dma_start(
+                out=frames[h][:].bitcast(I32),
+                in_=frames_words.rearrange("g p b -> p g b")[:, :, h * M : (h + 1) * M].bitcast(I32),
+            )
+
+        def load_xref(jg, h):
+            r0 = jg * KP + h * 2 * P
+            nc.sync.dma_start(out=xref_raw[jg, h][:], in_=xref[r0 : r0 + 2 * P, :].rearrange("(a p) d -> p a d", p=P))
+
+        def load_jac(cc, g):
+            nc.sync.dma_start(
+                out=jac_raw[cc, g][:],
+                in_=jac[g * KP : (g + 1) * KP, cc * CC : (cc + 1) * CC].rearrange("(p t) c -> p t c", t=PACK),
+            )
+
+        def sort_refs(jg):
+            src = refs_raw[:].bitcast(I32)[:, :, jg * 256 : (jg + 1) * 256]
+            nc.vector.tensor_copy(
+                out=refs[jg][:].bitcast(I32).rearrange("p g (t q w) -> p g t q w", t=PACK, w=4),
+                in_=src.rearrange("p g (q t w) -> p g t q w", t=PACK, w=4),
+            )
+            src = refs_sc_raw[:].bitcast(I32)[:, :, jg * 128 : (jg + 1) * 128]
+            nc.vector.tensor_copy(
+                out=refs_sc[jg][:].bitcast(I32).rearrange("p g (t q w) -> p g t q w", t=PACK, w=2),
+                in_=src.rearrange("p g (q t w) -> p g t q w", t=PACK, w=2),
+            )
+
+        def similarities(mc):
+            sq = ring.tile([P, 2, 2, MC, 2], F32, name="squares", align_bytes=64)
+            squares[mc] = sq
+            fr = frames[mc // 2]
+            b0 = (mc % 2) * 2 * MC
+            for jg in range(2):
+                for pair in range(2):
+                    bank = new_bank()
+                    for e in range(2):
+                        t = 2 * pair + e
+                        for g in range(2):
+                            nc.tensor.matmul_mx(
+                                out=bank[:, e * MC : (e + 1) * MC],
+                                lhsT=refs[jg][:, g, t * 256 : (t + 1) * 256].bitcast(FP4X4),
+                                lhsT_scale=refs_sc[jg][:, g, t * P : (t + 1) * P],
+                                rhs=fr[:, g, b0 : b0 + 2 * MC].bitcast(FP4X4),
+                                rhs_scale=frames_sc[:, g, mc * MC : (mc + 1) * MC],
+                                start=(g == 0),
+                                stop=(g == 1),
+                            )
+                    nc.scalar.activation(
+                        out=sq[:, jg, pair], in_=bank[:].rearrange("p (e n) -> p n e", e=2), func=SQUARE
+                    )
+
+        def slopes(mc, jg):
+            if jg == 0:
+                h_bf[mc] = ring.tile([P, 2, MC, PACK], BF16, name="h_bf", align_bytes=64)
+            nc.vector.tensor_tensor(
+                out=h_bf[mc][:, jg].rearrange("p n (a e) -> p n a e", e=2),
+                in0=squares[mc][:, jg].rearrange("p a n e -> p n a e"),
+                in1=coef_slot[:, jg].rearrange("p (a e) -> p a e", e=2).unsqueeze(1).to_broadcast([P, MC, 2, 2]),
+                op=MULT,
+            )
+
+        def quantize_h(mc):
+            quantize(h_q[mc], h_bf[mc][:].rearrange("p g n t -> p (g n t)"))
+
+        def turn_xref(jg):
+            for g in range(2):
+                xref_bf[jg, g] = ring.tile([P, PACK * P * PACK], BF16, name="xref_bf", bufs=4, align_bytes=64)
+            for h in range(2):
+                words = xref_raw[jg, h][:].bitcast(F32)
+                for g in range(2):
+                    bank = new_bank()
+                    for u in range(2):
+                        for a in range(2):
+                            c0 = (2 * u + a) * P
+                            nc.tensor.transpose(
+                                bank[:, c0 : c0 + P], words[:, a, 256 * g + u : 256 * (g + 1) : 2], ident[:]
+                            )
+                    dst = xref_bf[jg, g][:].bitcast(F32).rearrange("p (t h q r u) -> p h t q r u", t=PACK, h=2, r=8, u=2)
+                    nc.scalar.copy(out=dst[:, h], in_=bank[:].rearrange("p (u q t r) -> p t q r u", u=2, t=PACK, r=8))
+
+        def interleave_jac(cc, g, half, on_vector):
+            if half == 0:
+                jac_bf[cc, g] = ring.tile([P, CC, PACK], BF16, name="jac_bf", bufs=3, align_bytes=64)
+            cols = slice(half * CC // 2, (half + 1) * CC // 2)
+            dst = jac_bf[cc, g][:, cols, :].rearrange("p (c i) t -> p c t i", i=4)
+            src = jac_raw[cc, g][:, :, cols].rearrange("p t (c i) -> p c t i", i=4)
+            if on_vector:
+                nc.vector.tensor_copy(out=dst, in_=src)
+            else:
+                nc.scalar.copy(out=dst, in_=src)
+
+        def quantize_jac(cc, g):
+            quantize(jac_q[cc, g], jac_bf[cc, g][:].rearrange("p c t -> p (c t)"))
+
+        def project(cc, jg, n):
+            if n == 0:
+                v_bf[cc, jg] = ring.tile([P, CC, PACK], BF16, name="v_bf", bufs=3, align_bytes=64)
+            bank = new_bank()
+            cols = slice(n * P, (n + 1) * P)
+            for t in range(PACK):
+                slot = slice(t * P, (t + 1) * P)
+                for g in range(2):
+                    nc.tensor.matmul_mx(
+                        out=bank[:, slot],
+                        lhsT=xref_q[jg, g][0][:, slot].bitcast(FP8X4),
+                        lhsT_scale=xref_q[jg, g][1][:, slot],
+                        rhs=jac_q[cc, g][0][:, cols].bitcast(FP8X4),
+                        rhs_scale=jac_q[cc, g][1][:, cols],
+                        start=(g == 0),
+                        stop=(g == 1),
+                    )
+            nc.scalar.copy(out=v_bf[cc, jg][:, cols, :], in_=bank[:].rearrange("p (t n) -> p n t", t=PACK))
+
+        def quantize_v(cc, jg):
+            quantize(v_q[cc, jg], v_bf[cc, jg][:].rearrange("p c t -> p (c t)"))
+
+        def forces(cc, mt):
+            bank = new_bank()
+            codes, scales = h_q[mt // 2]
+            for jg in range(2):
+                c0 = jg * MC + (mt % 2) * P
+                nc.tensor.matmul_mx(
+                    out=bank[:],
+                    lhsT=codes[:, c0 : c0 + P].bitcast(FP8X4),
+                    lhsT_scale=scales[:, c0 : c0 + P],
+                    rhs=v_q[cc, jg][0][:].bitcast(FP8X4),
+                    rhs_scale=v_q[cc, jg][1][:],
+                    start=(jg == 0),
+                    stop=(jg == 1),
+                )
+            res = ring.tile([P, CC], F32, name="res", bufs=8, align_bytes=64)
+            cols = slice(cc * CC, (cc + 1) * CC)
+            nc.vector.tensor_tensor(out=res[:], in0=bank[:], in1=base_rows[:, cols], op=ADD)
+            nc.sync.dma_start(out=out[mt * P : (mt + 1) * P, cols], in_=res[:])
+
+        nc.vector.memset(refs_sc_raw[:].bitcast(I32), 0)
+        nc.vector.memset(frames_sc[:].bitcast(I32), 0)
+        nc.vector.memset(coef_wide[:], 0.0)
+        nc.gpsimd.dma_start(
+            out=coef_rows[:].rearrange("t (a r) -> t a r", r=8), in_=coef.rearrange("(a t r) -> t a r", t=PACK, r=8)
+        )
+        load_scale_rows(nc.gpsimd, frames_sc, frames_scales)
+        make_identity(nc, ident[:])
+
+        nc.sync.dma_start(out=refs_raw[:].bitcast(I32), in_=refs_words.rearrange("g p b -> p g b").bitcast(I32))
+        load_frames(0)
+        load_scale_rows(nc.sync, refs_sc_raw, refs_scales)
+        load_jac(0, 0)
+        load_jac(0, 1)
+        load_xref(0, 0)
+        load_xref(0, 1)
+        load_frames(1)
+        load_xref(1, 0)
+        load_xref(1, 1)
+        for cc in (1, 2):
+            load_jac(cc, 0)
+            load_jac(cc, 1)
+        nc.sync.dma_start(out=base_rows[:], in_=base.partition_broadcast(P))
+
+        sort_refs(0)
+        sort_refs(1)
+        similarities(0)
+
+        nc.vector.tensor_copy(out=coef_wide[0:PACK, :], in_=coef_rows[:])
+        bank = new_bank()
+        for jg in range(2):
+            nc.tensor.transpose(bank[:, jg * P : (jg + 1) * P], coef_wide[:, jg * P : (jg + 1) * P], ident[:])
+        similarities(1)
+        for half in range(2):
+            interleave_jac(0, 0, half, True)
+        nc.vector.tensor_copy(
+            out=coef_slot[:], in_=bank[:, 0 : 2 * P].rearrange("p (g k) -> p g k", g=2)[:, :, 0:PACK]
+        )
+        for half in range(2):
+            interleave_jac(0, 1, half, True)
+        quantize_jac(0, 0)
+        slopes(0, 0)
+        quantize_jac(0, 1)
+        slopes(0, 1)
+        slopes(1, 0)
+        quantize_h(0)
+        slopes(1, 1)
+        turn_xref(0)
+        quantize(xref_q[0, 0], xref_bf[0, 0][:])
+        quantize_h(1)
+        quantize(xref_q[0, 1], xref_bf[0, 1][:])
+        similarities(2)
+        turn_xref(1)
+        for n in range(4):
+            project(0, 0, n)
+        for half in range(2):
+            interleave_jac(1, 0, half, True)
+        quantize(xref_q[1, 0], xref_bf[1, 0][:])
+        quantize(xref_q[1, 1], xref_bf[1, 1][:])
+        for half in range(2):
+            interleave_jac(1, 1, half, True)
+        for n in range(4):
+            project(0, 1, n)
+        quantize_jac(1, 0)
+        quantize_v(0, 0)
+        quantize_jac(1, 1)
+        slopes(2, 0)
+        project(1, 0, 0)
+        project(1, 0, 1)
+        quantize_v(0, 1)
+        project(1, 0, 2)
+        slopes(2, 1)
+
+        forces(0, 0)
+        interleave_jac(2, 0, 0, False)
+        project(1, 0, 3)
+        quantize_h(2)
+        forces(0, 1)
+        interleave_jac(2, 0, 1, False)
+        project(1, 1, 0)
+        quantize_v(1, 0)
+        forces(0, 2)
+        interleave_jac(2, 1, 0, False)
+        project(1, 1, 1)
+        quantize_jac(2, 0)
+        forces(0, 3)
+        project(1, 1, 2)
+        interleave_jac(2, 1, 1, True)
+        forces(0, 4)
+        project(1, 1, 3)
+        forces(0, 5)
+        quantize_jac(2, 1)
+        quantize_v(1, 1)
+        similarities(3)
+
+        for k in range(8):
+            project(2, k // 4, k % 4)
+            if k < 6:
+                forces(1, k)
+            if k < 2:
+                slopes(3, k)
+            if k == 3:
+                quantize_h(3)
+            if k == 4:
+                quantize_v(2, 0)
+        forces(0, 6)
+        quantize_v(2, 1)
+        forces(0, 7)
+        forces(1, 6)
+        forces(1, 7)
+        for mt in range(8):
+            forces(2, mt)

@@ -23,6 +23,7 @@ KP = 512
 BANK = 512
 MC = 256
 CC = 512
+V_CHUNKS = ((0, 512), (512, 512), (1024, 256), (1280, 256))
 
 
 def tile_cubic_kernel_forces_s12_kernel(
@@ -55,12 +56,12 @@ def tile_cubic_kernel_forces_s12_kernel(
         xref_raw = {(jg, h): kept("xref_raw%d%d" % (jg, h), [P, 2, D], BF16) for jg in range(2) for h in range(2)}
         jac_raw = {(cc, g): kept("jac_raw%d%d" % (cc, g), [P, PACK, CC], BF16) for cc in range(3) for g in range(2)}
 
-        def mx_pair(name):
-            return kept(name + "_codes", [P, 512], U32), kept(name + "_scales", [P, 512], U8)
+        def mx_pair(name, width=512):
+            return kept(name + "_codes", [P, width], U32), kept(name + "_scales", [P, width], U8)
 
         xref_q = {(jg, g): mx_pair("xref_q%d%d" % (jg, g)) for jg in range(2) for g in range(2)}
         jac_q = {(cc, g): mx_pair("jac_q%d%d" % (cc, g)) for cc in range(3) for g in range(2)}
-        v_q = {(cc, jg): mx_pair("v_q%d%d" % (cc, jg)) for cc in range(3) for jg in range(2)}
+        v_q = {(vc, jg): mx_pair("v_q%d%d" % (vc, jg), V_CHUNKS[vc][1]) for vc in range(4) for jg in range(2)}
         h_q = [mx_pair("h_q%d" % mc) for mc in range(4)]
 
         squares, h_bf, xref_bf, jac_bf, v_bf = {}, {}, {}, {}, {}
@@ -74,8 +75,8 @@ def tile_cubic_kernel_forces_s12_kernel(
             for r in range(4):
                 queue.dma_start(out=plane[:].bitcast(I32)[r:P:32], in_=rows[r].bitcast(I32))
 
-        def load_frames(h):
-            nc.sync.dma_start(
+        def load_frames(queue, h):
+            queue.dma_start(
                 out=frames[h][:].bitcast(I32),
                 in_=frames_words.rearrange("g p b -> p g b")[:, :, h * M : (h + 1) * M].bitcast(I32),
             )
@@ -169,11 +170,13 @@ def tile_cubic_kernel_forces_s12_kernel(
         def quantize_jac(cc, g):
             quantize(jac_q[cc, g], jac_bf[cc, g][:].rearrange("p c t -> p (c t)"))
 
-        def project(cc, jg, n):
+        def project(vc, jg, n):
+            c0, width = V_CHUNKS[vc]
             if n == 0:
-                v_bf[cc, jg] = ring.tile([P, CC, PACK], BF16, name="v_bf", bufs=3, align_bytes=64)
+                v_bf[vc, jg] = ring.tile([P, width, PACK], BF16, name="v_bf", bufs=3, align_bytes=64)
             bank = new_bank()
-            cols = slice(n * P, (n + 1) * P)
+            cc, first = divmod(c0 + n * P, CC)
+            cols = slice(first, first + P)
             for t in range(PACK):
                 slot = slice(t * P, (t + 1) * P)
                 for g in range(2):
@@ -186,47 +189,56 @@ def tile_cubic_kernel_forces_s12_kernel(
                         start=(g == 0),
                         stop=(g == 1),
                     )
-            nc.scalar.copy(out=v_bf[cc, jg][:, cols, :], in_=bank[:].rearrange("p (t n) -> p n t", t=PACK))
+            nc.scalar.copy(
+                out=v_bf[vc, jg][:, n * P : (n + 1) * P, :], in_=bank[:].rearrange("p (t n) -> p n t", t=PACK)
+            )
 
-        def quantize_v(cc, jg):
-            quantize(v_q[cc, jg], v_bf[cc, jg][:].rearrange("p c t -> p (c t)"))
+        def quantize_v(vc, jg):
+            quantize(v_q[vc, jg], v_bf[vc, jg][:].rearrange("p c t -> p (c t)"))
 
-        def forces(cc, mt):
+        def forces(vc, mt, tiles=1):
+            c0, width = V_CHUNKS[vc]
             bank = new_bank()
             codes, scales = h_q[mt // 2]
-            for jg in range(2):
-                c0 = jg * MC + (mt % 2) * P
-                nc.tensor.matmul_mx(
-                    out=bank[:],
-                    lhsT=codes[:, c0 : c0 + P].bitcast(FP8X4),
-                    lhsT_scale=scales[:, c0 : c0 + P],
-                    rhs=v_q[cc, jg][0][:].bitcast(FP8X4),
-                    rhs_scale=v_q[cc, jg][1][:],
-                    start=(jg == 0),
-                    stop=(jg == 1),
-                )
-            res = ring.tile([P, CC], F32, name="res", bufs=8, align_bytes=64)
-            cols = slice(cc * CC, (cc + 1) * CC)
-            nc.vector.tensor_tensor(out=res[:], in0=bank[:], in1=base_rows[:, cols], op=ADD)
-            nc.sync.dma_start(out=out[mt * P : (mt + 1) * P, cols], in_=res[:])
+            for a in range(tiles):
+                for jg in range(2):
+                    m0 = jg * MC + (mt % 2 + a) * P
+                    nc.tensor.matmul_mx(
+                        out=bank[:, a * width : (a + 1) * width],
+                        lhsT=codes[:, m0 : m0 + P].bitcast(FP8X4),
+                        lhsT_scale=scales[:, m0 : m0 + P],
+                        rhs=v_q[vc, jg][0][:].bitcast(FP8X4),
+                        rhs_scale=v_q[vc, jg][1][:],
+                        start=(jg == 0),
+                        stop=(jg == 1),
+                    )
+            res = ring.tile([P, tiles, width], F32, name="res", bufs=8, align_bytes=64)
+            nc.vector.tensor_tensor(
+                out=res[:],
+                in0=bank[:, 0 : tiles * width].rearrange("p (a c) -> p a c", a=tiles),
+                in1=base_rows[:, c0 : c0 + width].unsqueeze(1).to_broadcast([P, tiles, width]),
+                op=ADD,
+            )
+            rows = out[mt * P : (mt + tiles) * P, c0 : c0 + width]
+            nc.sync.dma_start(out=rows.rearrange("(a p) c -> p a c", p=P), in_=res[:])
 
-        nc.vector.memset(refs_sc_raw[:].bitcast(I32), 0)
+        nc.gpsimd.memset(refs_sc_raw[:].bitcast(I32), 0)
         nc.vector.memset(frames_sc[:].bitcast(I32), 0)
         nc.vector.memset(coef_wide[:], 0.0)
-        nc.gpsimd.dma_start(
-            out=coef_rows[:].rearrange("t (a r) -> t a r", r=8), in_=coef.rearrange("(a t r) -> t a r", t=PACK, r=8)
-        )
-        load_scale_rows(nc.gpsimd, frames_sc, frames_scales)
         make_identity(nc, ident[:])
 
-        nc.sync.dma_start(out=refs_raw[:].bitcast(I32), in_=refs_words.rearrange("g p b -> p g b").bitcast(I32))
-        load_frames(0)
         load_scale_rows(nc.sync, refs_sc_raw, refs_scales)
+        nc.scalar.dma_start(out=refs_raw[:].bitcast(I32), in_=refs_words.rearrange("g p b -> p g b").bitcast(I32))
+        load_frames(nc.scalar, 0)
+        load_scale_rows(nc.sync, frames_sc, frames_scales)
         load_jac(0, 0)
+        nc.sync.dma_start(
+            out=coef_rows[:].rearrange("t (a r) -> t a r", r=8), in_=coef.rearrange("(a t r) -> t a r", t=PACK, r=8)
+        )
         load_jac(0, 1)
         load_xref(0, 0)
         load_xref(0, 1)
-        load_frames(1)
+        load_frames(nc.sync, 1)
         load_xref(1, 0)
         load_xref(1, 1)
         for cc in (1, 2):
@@ -238,13 +250,13 @@ def tile_cubic_kernel_forces_s12_kernel(
         sort_refs(1)
         similarities(0)
 
+        for half in range(2):
+            interleave_jac(0, 0, half, True)
         nc.vector.tensor_copy(out=coef_wide[0:PACK, :], in_=coef_rows[:])
         bank = new_bank()
         for jg in range(2):
             nc.tensor.transpose(bank[:, jg * P : (jg + 1) * P], coef_wide[:, jg * P : (jg + 1) * P], ident[:])
         similarities(1)
-        for half in range(2):
-            interleave_jac(0, 0, half, True)
         nc.vector.tensor_copy(
             out=coef_slot[:], in_=bank[:, 0 : 2 * P].rearrange("p (g k) -> p g k", g=2)[:, :, 0:PACK]
         )
@@ -305,20 +317,35 @@ def tile_cubic_kernel_forces_s12_kernel(
         quantize_v(1, 1)
         similarities(3)
 
-        for k in range(8):
-            project(2, k // 4, k % 4)
-            if k < 6:
-                forces(1, k)
-            if k < 2:
-                slopes(3, k)
-            if k == 3:
-                quantize_h(3)
-            if k == 4:
-                quantize_v(2, 0)
-        forces(0, 6)
+        project(2, 0, 0)
+        forces(1, 0)
+        slopes(3, 0)
+        project(2, 0, 1)
+        forces(1, 1)
+        slopes(3, 1)
+        project(2, 1, 0)
+        quantize_v(2, 0)
+        forces(1, 2)
+        quantize_h(3)
+        project(2, 1, 1)
+        forces(1, 3)
+        project(3, 0, 0)
+        forces(1, 4)
         quantize_v(2, 1)
+        forces(1, 5)
+        project(3, 0, 1)
+        forces(0, 6)
         forces(0, 7)
+        quantize_v(3, 0)
+        project(3, 1, 0)
         forces(1, 6)
         forces(1, 7)
-        for mt in range(8):
-            forces(2, mt)
+        project(3, 1, 1)
+        forces(2, 0, 2)
+        quantize_v(3, 1)
+        for mt in (2, 4, 6):
+            forces(2, mt, 2)
+        for mt in (0, 2, 4):
+            forces(3, mt, 2)
+        forces(3, 6)
+        forces(3, 7)

@@ -81,9 +81,9 @@ def tile_cubic_kernel_forces_s12_kernel(
                 in_=frames_words.rearrange("g p b -> p g b")[:, :, h * M : (h + 1) * M].bitcast(I32),
             )
 
-        def load_xref(jg, h):
+        def load_xref(queue, jg, h):
             r0 = jg * KP + h * 2 * P
-            nc.sync.dma_start(out=xref_raw[jg, h][:], in_=xref[r0 : r0 + 2 * P, :].rearrange("(a p) d -> p a d", p=P))
+            queue.dma_start(out=xref_raw[jg, h][:], in_=xref[r0 : r0 + 2 * P, :].rearrange("(a p) d -> p a d", p=P))
 
         def load_jac(cc, g):
             nc.sync.dma_start(
@@ -103,29 +103,31 @@ def tile_cubic_kernel_forces_s12_kernel(
                 in_=src.rearrange("p g (q t w) -> p g t q w", t=PACK, w=2),
             )
 
-        def similarities(mc):
-            sq = ring.tile([P, 2, 2, MC, 2], F32, name="squares", align_bytes=64)
-            squares[mc] = sq
-            fr = frames[mc // 2]
+        def similarity_bank(mc, jg, pair):
+            if jg == 0 and pair == 0:
+                squares[mc] = ring.tile([P, 2, 2, MC, 2], F32, name="squares", align_bytes=64)
             b0 = (mc % 2) * 2 * MC
+            bank = new_bank()
+            for e in range(2):
+                t = 2 * pair + e
+                for g in range(2):
+                    nc.tensor.matmul_mx(
+                        out=bank[:, e * MC : (e + 1) * MC],
+                        lhsT=refs[jg][:, g, t * 256 : (t + 1) * 256].bitcast(FP4X4),
+                        lhsT_scale=refs_sc[jg][:, g, t * P : (t + 1) * P],
+                        rhs=frames[mc // 2][:, g, b0 : b0 + 2 * MC].bitcast(FP4X4),
+                        rhs_scale=frames_sc[:, g, mc * MC : (mc + 1) * MC],
+                        start=(g == 0),
+                        stop=(g == 1),
+                    )
+            nc.scalar.activation(
+                out=squares[mc][:, jg, pair], in_=bank[:].rearrange("p (e n) -> p n e", e=2), func=SQUARE
+            )
+
+        def similarities(mc):
             for jg in range(2):
                 for pair in range(2):
-                    bank = new_bank()
-                    for e in range(2):
-                        t = 2 * pair + e
-                        for g in range(2):
-                            nc.tensor.matmul_mx(
-                                out=bank[:, e * MC : (e + 1) * MC],
-                                lhsT=refs[jg][:, g, t * 256 : (t + 1) * 256].bitcast(FP4X4),
-                                lhsT_scale=refs_sc[jg][:, g, t * P : (t + 1) * P],
-                                rhs=fr[:, g, b0 : b0 + 2 * MC].bitcast(FP4X4),
-                                rhs_scale=frames_sc[:, g, mc * MC : (mc + 1) * MC],
-                                start=(g == 0),
-                                stop=(g == 1),
-                            )
-                    nc.scalar.activation(
-                        out=sq[:, jg, pair], in_=bank[:].rearrange("p (e n) -> p n e", e=2), func=SQUARE
-                    )
+                    similarity_bank(mc, jg, pair)
 
         def slopes(mc, jg):
             if jg == 0:
@@ -157,7 +159,7 @@ def tile_cubic_kernel_forces_s12_kernel(
                     nc.scalar.copy(out=dst[:, h], in_=bank[:].rearrange("p (u q t r) -> p t q r u", u=2, t=PACK, r=8))
 
         def interleave_jac(cc, g, half, on_vector):
-            if half == 0:
+            if (cc, g) not in jac_bf:
                 jac_bf[cc, g] = ring.tile([P, CC, PACK], BF16, name="jac_bf", bufs=3, align_bytes=64)
             cols = slice(half * CC // 2, (half + 1) * CC // 2)
             dst = jac_bf[cc, g][:, cols, :].rearrange("p (c i) t -> p c t i", i=4)
@@ -223,110 +225,114 @@ def tile_cubic_kernel_forces_s12_kernel(
             nc.sync.dma_start(out=rows.rearrange("(a p) c -> p a c", p=P), in_=res[:])
 
         nc.gpsimd.memset(refs_sc_raw[:].bitcast(I32), 0)
-        nc.vector.memset(frames_sc[:].bitcast(I32), 0)
         nc.vector.memset(coef_wide[:], 0.0)
+        nc.vector.memset(frames_sc[:].bitcast(I32), 0)
         make_identity(nc, ident[:])
 
-        load_scale_rows(nc.sync, refs_sc_raw, refs_scales)
-        nc.scalar.dma_start(out=refs_raw[:].bitcast(I32), in_=refs_words.rearrange("g p b -> p g b").bitcast(I32))
-        load_frames(nc.scalar, 0)
-        load_scale_rows(nc.sync, frames_sc, frames_scales)
-        load_jac(0, 0)
         nc.sync.dma_start(
             out=coef_rows[:].rearrange("t (a r) -> t a r", r=8), in_=coef.rearrange("(a t r) -> t a r", t=PACK, r=8)
         )
+        load_scale_rows(nc.sync, refs_sc_raw, refs_scales)
+        load_xref(nc.scalar, 0, 0)
+        load_xref(nc.sync, 0, 1)
+        nc.sync.dma_start(out=refs_raw[:].bitcast(I32), in_=refs_words.rearrange("g p b -> p g b").bitcast(I32))
+        load_frames(nc.sync, 0)
+        load_scale_rows(nc.sync, frames_sc, frames_scales)
+        load_jac(0, 0)
         load_jac(0, 1)
-        load_xref(0, 0)
-        load_xref(0, 1)
+        load_xref(nc.sync, 1, 0)
+        load_xref(nc.sync, 1, 1)
         load_frames(nc.sync, 1)
-        load_xref(1, 0)
-        load_xref(1, 1)
         for cc in (1, 2):
             load_jac(cc, 0)
             load_jac(cc, 1)
         nc.sync.dma_start(out=base_rows[:], in_=base.partition_broadcast(P))
 
-        sort_refs(0)
-        sort_refs(1)
-        similarities(0)
-
-        for half in range(2):
-            interleave_jac(0, 0, half, True)
         nc.vector.tensor_copy(out=coef_wide[0:PACK, :], in_=coef_rows[:])
         bank = new_bank()
         for jg in range(2):
             nc.tensor.transpose(bank[:, jg * P : (jg + 1) * P], coef_wide[:, jg * P : (jg + 1) * P], ident[:])
-        similarities(1)
         nc.vector.tensor_copy(
             out=coef_slot[:], in_=bank[:, 0 : 2 * P].rearrange("p (g k) -> p g k", g=2)[:, :, 0:PACK]
         )
-        for half in range(2):
-            interleave_jac(0, 1, half, True)
+        turn_xref(0)
+        sort_refs(0)
+        sort_refs(1)
+        quantize(xref_q[0, 0], xref_bf[0, 0][:])
+        quantize(xref_q[0, 1], xref_bf[0, 1][:])
+        interleave_jac(0, 0, 1, False)
+        similarities(0)
+        similarities(1)
+        interleave_jac(0, 0, 0, True)
+        interleave_jac(0, 1, 0, True)
+        interleave_jac(0, 1, 1, True)
         quantize_jac(0, 0)
         slopes(0, 0)
         quantize_jac(0, 1)
         slopes(0, 1)
         slopes(1, 0)
         quantize_h(0)
-        slopes(1, 1)
-        turn_xref(0)
-        quantize(xref_q[0, 0], xref_bf[0, 0][:])
-        quantize_h(1)
-        quantize(xref_q[0, 1], xref_bf[0, 1][:])
-        similarities(2)
         turn_xref(1)
-        for n in range(4):
-            project(0, 0, n)
-        for half in range(2):
-            interleave_jac(1, 0, half, True)
+        interleave_jac(1, 0, 0, True)
+        project(0, 0, 0)
+        project(0, 0, 1)
         quantize(xref_q[1, 0], xref_bf[1, 0][:])
         quantize(xref_q[1, 1], xref_bf[1, 1][:])
-        for half in range(2):
-            interleave_jac(1, 1, half, True)
-        for n in range(4):
-            project(0, 1, n)
+        project(0, 0, 2)
+        project(0, 0, 3)
+        interleave_jac(1, 0, 1, True)
+        interleave_jac(1, 1, 0, True)
         quantize_jac(1, 0)
+        interleave_jac(1, 1, 1, True)
+        project(0, 1, 0)
+        project(0, 1, 1)
+        project(0, 1, 2)
+        project(0, 1, 3)
         quantize_v(0, 0)
         quantize_jac(1, 1)
-        slopes(2, 0)
+        slopes(1, 1)
+        similarities(2)
+        quantize_v(0, 1)
+        quantize_h(1)
         project(1, 0, 0)
         project(1, 0, 1)
-        quantize_v(0, 1)
-        project(1, 0, 2)
-        slopes(2, 1)
-
-        forces(0, 0)
         interleave_jac(2, 0, 0, False)
-        project(1, 0, 3)
-        quantize_h(2)
+        slopes(2, 0)
+        forces(0, 0)
+        project(1, 0, 2)
         forces(0, 1)
+        slopes(2, 1)
         interleave_jac(2, 0, 1, False)
-        project(1, 1, 0)
-        quantize_v(1, 0)
+        project(1, 0, 3)
         forces(0, 2)
+        quantize_h(2)
+        project(1, 1, 0)
         interleave_jac(2, 1, 0, False)
+        forces(0, 3)
+        quantize_v(1, 0)
         project(1, 1, 1)
         quantize_jac(2, 0)
-        forces(0, 3)
-        project(1, 1, 2)
-        interleave_jac(2, 1, 1, True)
         forces(0, 4)
-        project(1, 1, 3)
+        project(1, 1, 2)
+        interleave_jac(2, 1, 1, False)
         forces(0, 5)
+        project(1, 1, 3)
         quantize_jac(2, 1)
+        similarity_bank(3, 0, 0)
+        similarity_bank(3, 0, 1)
         quantize_v(1, 1)
-        similarities(3)
-
+        similarity_bank(3, 1, 0)
+        similarity_bank(3, 1, 1)
+        slopes(3, 0)
         project(2, 0, 0)
         forces(1, 0)
-        slopes(3, 0)
+        slopes(3, 1)
         project(2, 0, 1)
         forces(1, 1)
-        slopes(3, 1)
         project(2, 1, 0)
         quantize_v(2, 0)
-        forces(1, 2)
         quantize_h(3)
+        forces(1, 2)
         project(2, 1, 1)
         forces(1, 3)
         project(3, 0, 0)
@@ -343,9 +349,11 @@ def tile_cubic_kernel_forces_s12_kernel(
         project(3, 1, 1)
         forces(2, 0, 2)
         quantize_v(3, 1)
-        for mt in (2, 4, 6):
-            forces(2, mt, 2)
-        for mt in (0, 2, 4):
-            forces(3, mt, 2)
+        forces(2, 2, 2)
+        forces(2, 4, 2)
+        forces(2, 6, 2)
+        forces(3, 0, 2)
+        forces(3, 2, 2)
+        forces(3, 4, 2)
         forces(3, 6)
         forces(3, 7)

@@ -18,12 +18,18 @@ MULT = mybir.AluOpType.mult
 ADD = mybir.AluOpType.add
 
 P = 128
-PACK = 4
-KP = 512
+SLOTS = 4
+K_PASS = P * SLOTS
+PASSES = 2
+RUN = 8
 BANK = 512
-MC = 256
-CC = 512
-V_CHUNKS = ((0, 512), (512, 512), (1024, 256), (1280, 256))
+BANKS = 8
+GROUP = 256
+GROUPS = M // GROUP
+JAC_COLS = 512
+JAC_CHUNKS = C // JAC_COLS
+V_PIECES = ((0, 512), (512, 512), (1024, 256), (1280, 256))
+LOW, HIGH, WHOLE = slice(0, JAC_COLS // 2), slice(JAC_COLS // 2, JAC_COLS), slice(0, JAC_COLS)
 
 
 def tile_cubic_kernel_forces_s12_kernel(
@@ -33,36 +39,39 @@ def tile_cubic_kernel_forces_s12_kernel(
     with ExitStack() as ctx:
         keep = ctx.enter_context(tc.tile_pool(name="keep", bufs=1))
         ring = ctx.enter_context(tc.tile_pool(name="ring", bufs=2))
-        psum = ctx.enter_context(tc.psum_pool(name="psum", bufs=8))
+        psum = ctx.enter_context(tc.psum_pool(name="psum", bufs=BANKS))
         ctx.enter_context(tc.manual_schedule())
 
         def kept(name, shape, dtype):
             return keep.tile(shape, dtype, name=name, align_bytes=64)
 
+        def mx_pair(name, width):
+            return kept(name + "_codes", [P, width], U32), kept(name + "_scales", [P, width], U8)
+
         def new_bank():
             return psum.tile([P, BANK], F32, name="bank")
 
-        refs_raw = kept("refs_raw", [P, 2, 2 * J], U8)
-        refs_sc_raw = kept("refs_sc_raw", [P, 2, J], U8)
-        frames_sc = kept("frames_sc", [P, 2, M], U8)
-        frames = [kept("frames%d" % h, [P, 2, M], U8) for h in range(2)]
-        refs = [kept("refs%d" % jg, [P, 2, J], U8) for jg in range(2)]
-        refs_sc = [kept("refs_sc%d" % jg, [P, 2, KP], U8) for jg in range(2)]
-        coef_rows = kept("coef_rows", [PACK, 2 * P], BF16)
-        coef_wide = kept("coef_wide", [P, 2 * P], F32)
-        coef_slot = kept("coef_slot", [P, 2, PACK], F32)
+        two = range(PASSES)
+        refs_raw = kept("refs_raw", [P, PASSES, 2 * J], U8)
+        refs_plane_raw = kept("refs_plane_raw", [P, PASSES, J], U8)
+        frames_plane = kept("frames_plane", [P, PASSES, M], U8)
+        frames = [kept("frames%d" % h, [P, PASSES, M], U8) for h in range(2)]
+        refs = [kept("refs%d" % jg, [P, PASSES, 2 * K_PASS], U8) for jg in two]
+        refs_plane = [kept("refs_plane%d" % jg, [P, PASSES, K_PASS], U8) for jg in two]
+        coef_rows = kept("coef_rows", [SLOTS, PASSES * P], BF16)
+        coef_wide = kept("coef_wide", [P, PASSES * P], F32)
+        coef_slot = kept("coef_slot", [P, PASSES, SLOTS], F32)
         ident = kept("ident", [P, P], F32)
         base_rows = kept("base_rows", [P, C], BF16)
-        xref_raw = {(jg, h): kept("xref_raw%d%d" % (jg, h), [P, 2, D], BF16) for jg in range(2) for h in range(2)}
-        jac_raw = {(cc, g): kept("jac_raw%d%d" % (cc, g), [P, PACK, CC], BF16) for cc in range(3) for g in range(2)}
+        xref_raw = {(jg, h): kept("xref_raw%d%d" % (jg, h), [P, 2, D], BF16) for jg in two for h in range(2)}
+        jac_raw = {
+            (cc, g): kept("jac_raw%d%d" % (cc, g), [P, SLOTS, JAC_COLS], BF16) for cc in range(JAC_CHUNKS) for g in two
+        }
 
-        def mx_pair(name, width=512):
-            return kept(name + "_codes", [P, width], U32), kept(name + "_scales", [P, width], U8)
-
-        xref_q = {(jg, g): mx_pair("xref_q%d%d" % (jg, g)) for jg in range(2) for g in range(2)}
-        jac_q = {(cc, g): mx_pair("jac_q%d%d" % (cc, g)) for cc in range(3) for g in range(2)}
-        v_q = {(vc, jg): mx_pair("v_q%d%d" % (vc, jg), V_CHUNKS[vc][1]) for vc in range(4) for jg in range(2)}
-        h_q = [mx_pair("h_q%d" % mc) for mc in range(4)]
+        xref_q = {(jg, g): mx_pair("xref_q%d%d" % (jg, g), K_PASS) for jg in two for g in two}
+        jac_q = {(cc, g): mx_pair("jac_q%d%d" % (cc, g), JAC_COLS) for cc in range(JAC_CHUNKS) for g in two}
+        v_q = {(vc, jg): mx_pair("v_q%d%d" % (vc, jg), V_PIECES[vc][1]) for vc in range(len(V_PIECES)) for jg in two}
+        h_q = [mx_pair("h_q%d" % mg, PASSES * GROUP) for mg in range(GROUPS)]
 
         squares, h_bf, xref_bf, jac_bf, v_bf = {}, {}, {}, {}, {}
 
@@ -70,141 +79,151 @@ def tile_cubic_kernel_forces_s12_kernel(
             codes, scales = pair
             nc.vector.quantize_mx(out=codes[:].bitcast(FP8X4), scales=scales[:], in_=src)
 
-        def load_scale_rows(queue, plane, scales):
+        def load_scale_rows(plane, scales):
             rows = scales.rearrange("g (a r) n -> r a g n", r=4)
             for r in range(4):
-                queue.dma_start(out=plane[:].bitcast(I32)[r:P:32], in_=rows[r].bitcast(I32))
+                nc.sync.dma_start(out=plane[:].bitcast(I32)[r:P:32], in_=rows[r].bitcast(I32))
 
-        def load_frames(queue, h):
-            queue.dma_start(
+        def load_frames(h):
+            nc.sync.dma_start(
                 out=frames[h][:].bitcast(I32),
                 in_=frames_words.rearrange("g p b -> p g b")[:, :, h * M : (h + 1) * M].bitcast(I32),
             )
 
         def load_xref(queue, jg, h):
-            r0 = jg * KP + h * 2 * P
+            r0 = jg * K_PASS + h * 2 * P
             queue.dma_start(out=xref_raw[jg, h][:], in_=xref[r0 : r0 + 2 * P, :].rearrange("(a p) d -> p a d", p=P))
 
-        def load_jac(cc, g):
-            nc.sync.dma_start(
-                out=jac_raw[cc, g][:],
-                in_=jac[g * KP : (g + 1) * KP, cc * CC : (cc + 1) * CC].rearrange("(p t) c -> p t c", t=PACK),
-            )
+        def load_jac(cc):
+            for g in two:
+                rows = jac[g * K_PASS : (g + 1) * K_PASS, cc * JAC_COLS : (cc + 1) * JAC_COLS]
+                nc.sync.dma_start(out=jac_raw[cc, g][:], in_=rows.rearrange("(p t) c -> p t c", t=SLOTS))
 
         def sort_refs(jg):
-            src = refs_raw[:].bitcast(I32)[:, :, jg * 256 : (jg + 1) * 256]
-            nc.vector.tensor_copy(
-                out=refs[jg][:].bitcast(I32).rearrange("p g (t q w) -> p g t q w", t=PACK, w=4),
-                in_=src.rearrange("p g (q t w) -> p g t q w", t=PACK, w=4),
-            )
-            src = refs_sc_raw[:].bitcast(I32)[:, :, jg * 128 : (jg + 1) * 128]
-            nc.vector.tensor_copy(
-                out=refs_sc[jg][:].bitcast(I32).rearrange("p g (t q w) -> p g t q w", t=PACK, w=2),
-                in_=src.rearrange("p g (q t w) -> p g t q w", t=PACK, w=2),
-            )
+            for dst, src, words in ((refs[jg], refs_raw, 4), (refs_plane[jg], refs_plane_raw, 2)):
+                width = words * K_PASS // RUN
+                part = src[:].bitcast(I32)[:, :, jg * width : (jg + 1) * width]
+                nc.vector.tensor_copy(
+                    out=dst[:].bitcast(I32).rearrange("p g (t q w) -> p g t q w", t=SLOTS, w=words),
+                    in_=part.rearrange("p g (q t w) -> p g t q w", t=SLOTS, w=words),
+                )
 
-        def similarity_bank(mc, jg, pair):
+        def spread_coef():
+            nc.vector.tensor_copy(out=coef_wide[0:SLOTS, :], in_=coef_rows[:])
+            bank = new_bank()
+            for jg in two:
+                nc.tensor.transpose(bank[:, jg * P : (jg + 1) * P], coef_wide[:, jg * P : (jg + 1) * P], ident[:])
+            turned = bank[:, 0 : PASSES * P].rearrange("p (g k) -> p g k", g=PASSES)
+            nc.vector.tensor_copy(out=coef_slot[:], in_=turned[:, :, 0:SLOTS])
+
+        def similarity_bank(mg, jg, pair):
             if jg == 0 and pair == 0:
-                squares[mc] = ring.tile([P, 2, 2, MC, 2], F32, name="squares", align_bytes=64)
-            b0 = (mc % 2) * 2 * MC
+                squares[mg] = ring.tile([P, PASSES, 2, GROUP, 2], F32, name="squares", align_bytes=64)
+            b0 = (mg % 2) * 2 * GROUP
             bank = new_bank()
             for e in range(2):
                 t = 2 * pair + e
-                for g in range(2):
+                for g in two:
                     nc.tensor.matmul_mx(
-                        out=bank[:, e * MC : (e + 1) * MC],
-                        lhsT=refs[jg][:, g, t * 256 : (t + 1) * 256].bitcast(FP4X4),
-                        lhsT_scale=refs_sc[jg][:, g, t * P : (t + 1) * P],
-                        rhs=frames[mc // 2][:, g, b0 : b0 + 2 * MC].bitcast(FP4X4),
-                        rhs_scale=frames_sc[:, g, mc * MC : (mc + 1) * MC],
+                        out=bank[:, e * GROUP : (e + 1) * GROUP],
+                        lhsT=refs[jg][:, g, t * 2 * P : (t + 1) * 2 * P].bitcast(FP4X4),
+                        lhsT_scale=refs_plane[jg][:, g, t * P : (t + 1) * P],
+                        rhs=frames[mg // 2][:, g, b0 : b0 + 2 * GROUP].bitcast(FP4X4),
+                        rhs_scale=frames_plane[:, g, mg * GROUP : (mg + 1) * GROUP],
                         start=(g == 0),
-                        stop=(g == 1),
+                        stop=(g == PASSES - 1),
                     )
             nc.scalar.activation(
-                out=squares[mc][:, jg, pair], in_=bank[:].rearrange("p (e n) -> p n e", e=2), func=SQUARE
+                out=squares[mg][:, jg, pair], in_=bank[:].rearrange("p (e n) -> p n e", e=2), func=SQUARE
             )
 
-        def similarities(mc):
-            for jg in range(2):
+        def similarities(mg):
+            for jg in two:
                 for pair in range(2):
-                    similarity_bank(mc, jg, pair)
+                    similarity_bank(mg, jg, pair)
 
-        def slopes(mc, jg):
+        def slopes(mg, jg):
             if jg == 0:
-                h_bf[mc] = ring.tile([P, 2, MC, PACK], BF16, name="h_bf", align_bytes=64)
+                h_bf[mg] = ring.tile([P, PASSES, GROUP, SLOTS], BF16, name="h_bf", align_bytes=64)
+            factor = coef_slot[:, jg].rearrange("p (a e) -> p a e", e=2).unsqueeze(1)
             nc.vector.tensor_tensor(
-                out=h_bf[mc][:, jg].rearrange("p n (a e) -> p n a e", e=2),
-                in0=squares[mc][:, jg].rearrange("p a n e -> p n a e"),
-                in1=coef_slot[:, jg].rearrange("p (a e) -> p a e", e=2).unsqueeze(1).to_broadcast([P, MC, 2, 2]),
+                out=h_bf[mg][:, jg].rearrange("p n (a e) -> p n a e", e=2),
+                in0=squares[mg][:, jg].rearrange("p a n e -> p n a e"),
+                in1=factor.to_broadcast([P, GROUP, 2, 2]),
                 op=MULT,
             )
 
-        def quantize_h(mc):
-            quantize(h_q[mc], h_bf[mc][:].rearrange("p g n t -> p (g n t)"))
+        def quantize_h(mg):
+            quantize(h_q[mg], h_bf[mg][:].rearrange("p g n t -> p (g n t)"))
 
         def turn_xref(jg):
-            for g in range(2):
-                xref_bf[jg, g] = ring.tile([P, PACK * P * PACK], BF16, name="xref_bf", bufs=4, align_bytes=64)
+            for g in two:
+                xref_bf[jg, g] = ring.tile([P, K_PASS * SLOTS], BF16, name="xref_bf", bufs=4, align_bytes=64)
             for h in range(2):
                 words = xref_raw[jg, h][:].bitcast(F32)
-                for g in range(2):
+                for g in two:
                     bank = new_bank()
+                    w0 = g * K_PASS // 2
                     for u in range(2):
                         for a in range(2):
                             c0 = (2 * u + a) * P
                             nc.tensor.transpose(
-                                bank[:, c0 : c0 + P], words[:, a, 256 * g + u : 256 * (g + 1) : 2], ident[:]
+                                bank[:, c0 : c0 + P], words[:, a, w0 + u : w0 + K_PASS // 2 : 2], ident[:]
                             )
-                    dst = xref_bf[jg, g][:].bitcast(F32).rearrange("p (t h q r u) -> p h t q r u", t=PACK, h=2, r=8, u=2)
-                    nc.scalar.copy(out=dst[:, h], in_=bank[:].rearrange("p (u q t r) -> p t q r u", u=2, t=PACK, r=8))
+                    dst = xref_bf[jg, g][:].bitcast(F32)
+                    nc.scalar.copy(
+                        out=dst.rearrange("p (t h q r u) -> p h t q r u", t=SLOTS, h=2, r=RUN, u=2)[:, h],
+                        in_=bank[:].rearrange("p (u q t r) -> p t q r u", u=2, t=SLOTS, r=RUN),
+                    )
 
-        def interleave_jac(cc, g, half, on_vector):
+        def quantize_xref(jg):
+            for g in two:
+                quantize(xref_q[jg, g], xref_bf[jg, g][:])
+
+        def interleave_jac(copy, cc, g, cols):
             if (cc, g) not in jac_bf:
-                jac_bf[cc, g] = ring.tile([P, CC, PACK], BF16, name="jac_bf", bufs=3, align_bytes=64)
-            cols = slice(half * CC // 2, (half + 1) * CC // 2)
-            dst = jac_bf[cc, g][:, cols, :].rearrange("p (c i) t -> p c t i", i=4)
-            src = jac_raw[cc, g][:, :, cols].rearrange("p t (c i) -> p c t i", i=4)
-            if on_vector:
-                nc.vector.tensor_copy(out=dst, in_=src)
-            else:
-                nc.scalar.copy(out=dst, in_=src)
+                jac_bf[cc, g] = ring.tile([P, JAC_COLS, SLOTS], BF16, name="jac_bf", bufs=3, align_bytes=64)
+            copy(
+                out=jac_bf[cc, g][:, cols, :].rearrange("p (c i) t -> p c t i", i=4),
+                in_=jac_raw[cc, g][:, :, cols].rearrange("p t (c i) -> p c t i", i=4),
+            )
 
         def quantize_jac(cc, g):
             quantize(jac_q[cc, g], jac_bf[cc, g][:].rearrange("p c t -> p (c t)"))
 
         def project(vc, jg, n):
-            c0, width = V_CHUNKS[vc]
+            c0, width = V_PIECES[vc]
             if n == 0:
-                v_bf[vc, jg] = ring.tile([P, width, PACK], BF16, name="v_bf", bufs=3, align_bytes=64)
+                v_bf[vc, jg] = ring.tile([P, width, SLOTS], BF16, name="v_bf", bufs=3, align_bytes=64)
             bank = new_bank()
-            cc, first = divmod(c0 + n * P, CC)
+            cc, first = divmod(c0 + n * P, JAC_COLS)
             cols = slice(first, first + P)
-            for t in range(PACK):
-                slot = slice(t * P, (t + 1) * P)
-                for g in range(2):
+            for t in range(SLOTS):
+                quarter = slice(t * P, (t + 1) * P)
+                for g in two:
                     nc.tensor.matmul_mx(
-                        out=bank[:, slot],
-                        lhsT=xref_q[jg, g][0][:, slot].bitcast(FP8X4),
-                        lhsT_scale=xref_q[jg, g][1][:, slot],
+                        out=bank[:, quarter],
+                        lhsT=xref_q[jg, g][0][:, quarter].bitcast(FP8X4),
+                        lhsT_scale=xref_q[jg, g][1][:, quarter],
                         rhs=jac_q[cc, g][0][:, cols].bitcast(FP8X4),
                         rhs_scale=jac_q[cc, g][1][:, cols],
                         start=(g == 0),
-                        stop=(g == 1),
+                        stop=(g == PASSES - 1),
                     )
             nc.scalar.copy(
-                out=v_bf[vc, jg][:, n * P : (n + 1) * P, :], in_=bank[:].rearrange("p (t n) -> p n t", t=PACK)
+                out=v_bf[vc, jg][:, n * P : (n + 1) * P, :], in_=bank[:].rearrange("p (t n) -> p n t", t=SLOTS)
             )
 
         def quantize_v(vc, jg):
             quantize(v_q[vc, jg], v_bf[vc, jg][:].rearrange("p c t -> p (c t)"))
 
         def forces(vc, mt, tiles=1):
-            c0, width = V_CHUNKS[vc]
+            c0, width = V_PIECES[vc]
             bank = new_bank()
             codes, scales = h_q[mt // 2]
             for a in range(tiles):
-                for jg in range(2):
-                    m0 = jg * MC + (mt % 2 + a) * P
+                for jg in two:
+                    m0 = jg * GROUP + (mt % 2 + a) * P
                     nc.tensor.matmul_mx(
                         out=bank[:, a * width : (a + 1) * width],
                         lhsT=codes[:, m0 : m0 + P].bitcast(FP8X4),
@@ -212,9 +231,9 @@ def tile_cubic_kernel_forces_s12_kernel(
                         rhs=v_q[vc, jg][0][:].bitcast(FP8X4),
                         rhs_scale=v_q[vc, jg][1][:],
                         start=(jg == 0),
-                        stop=(jg == 1),
+                        stop=(jg == PASSES - 1),
                     )
-            res = ring.tile([P, tiles, width], F32, name="res", bufs=8, align_bytes=64)
+            res = ring.tile([P, tiles, width], F32, name="res", bufs=BANKS, align_bytes=64)
             nc.vector.tensor_tensor(
                 out=res[:],
                 in0=bank[:, 0 : tiles * width].rearrange("p (a c) -> p a c", a=tiles),
@@ -224,106 +243,95 @@ def tile_cubic_kernel_forces_s12_kernel(
             rows = out[mt * P : (mt + tiles) * P, c0 : c0 + width]
             nc.sync.dma_start(out=rows.rearrange("(a p) c -> p a c", p=P), in_=res[:])
 
-        nc.gpsimd.memset(refs_sc_raw[:].bitcast(I32), 0)
-        nc.vector.memset(coef_wide[:], 0.0)
-        nc.vector.memset(frames_sc[:].bitcast(I32), 0)
+        on_vector, on_scalar = nc.vector.tensor_copy, nc.scalar.copy
+
+        nc.gpsimd.memset(refs_plane_raw[:].bitcast(I32), 0)
+        nc.gpsimd.memset(frames_plane[:].bitcast(I32), 0)
+        nc.gpsimd.memset(coef_wide[:], 0.0)
         make_identity(nc, ident[:])
 
         nc.sync.dma_start(
-            out=coef_rows[:].rearrange("t (a r) -> t a r", r=8), in_=coef.rearrange("(a t r) -> t a r", t=PACK, r=8)
+            out=coef_rows[:].rearrange("t (a r) -> t a r", r=RUN),
+            in_=coef.rearrange("(a t r) -> t a r", t=SLOTS, r=RUN),
         )
-        load_scale_rows(nc.sync, refs_sc_raw, refs_scales)
+        load_scale_rows(refs_plane_raw, refs_scales)
         load_xref(nc.scalar, 0, 0)
         load_xref(nc.sync, 0, 1)
         nc.sync.dma_start(out=refs_raw[:].bitcast(I32), in_=refs_words.rearrange("g p b -> p g b").bitcast(I32))
-        load_frames(nc.sync, 0)
-        load_scale_rows(nc.sync, frames_sc, frames_scales)
-        load_jac(0, 0)
-        load_jac(0, 1)
+        load_frames(0)
+        load_scale_rows(frames_plane, frames_scales)
+        load_jac(0)
         load_xref(nc.sync, 1, 0)
         load_xref(nc.sync, 1, 1)
-        load_frames(nc.sync, 1)
-        for cc in (1, 2):
-            load_jac(cc, 0)
-            load_jac(cc, 1)
+        load_jac(1)
+        load_frames(1)
+        load_jac(2)
         nc.sync.dma_start(out=base_rows[:], in_=base.partition_broadcast(P))
 
-        nc.vector.tensor_copy(out=coef_wide[0:PACK, :], in_=coef_rows[:])
-        bank = new_bank()
-        for jg in range(2):
-            nc.tensor.transpose(bank[:, jg * P : (jg + 1) * P], coef_wide[:, jg * P : (jg + 1) * P], ident[:])
-        nc.vector.tensor_copy(
-            out=coef_slot[:], in_=bank[:, 0 : 2 * P].rearrange("p (g k) -> p g k", g=2)[:, :, 0:PACK]
-        )
+
+        spread_coef()
         turn_xref(0)
         sort_refs(0)
         sort_refs(1)
-        quantize(xref_q[0, 0], xref_bf[0, 0][:])
-        quantize(xref_q[0, 1], xref_bf[0, 1][:])
-        interleave_jac(0, 0, 1, False)
+        quantize_xref(0)
+
+        interleave_jac(on_scalar, 0, 0, HIGH)
         similarities(0)
         similarities(1)
-        interleave_jac(0, 0, 0, True)
-        interleave_jac(0, 1, 0, True)
-        interleave_jac(0, 1, 1, True)
+        interleave_jac(on_vector, 0, 0, LOW)
+        interleave_jac(on_vector, 0, 1, WHOLE)
         quantize_jac(0, 0)
         slopes(0, 0)
         quantize_jac(0, 1)
         slopes(0, 1)
         slopes(1, 0)
         quantize_h(0)
+
         turn_xref(1)
-        interleave_jac(1, 0, 0, True)
-        project(0, 0, 0)
-        project(0, 0, 1)
-        quantize(xref_q[1, 0], xref_bf[1, 0][:])
-        quantize(xref_q[1, 1], xref_bf[1, 1][:])
-        project(0, 0, 2)
-        project(0, 0, 3)
-        interleave_jac(1, 0, 1, True)
-        interleave_jac(1, 1, 0, True)
+        quantize_xref(1)
+        for n in range(4):
+            project(0, 0, n)
+        interleave_jac(on_vector, 1, 0, WHOLE)
+        interleave_jac(on_vector, 1, 1, WHOLE)
         quantize_jac(1, 0)
-        interleave_jac(1, 1, 1, True)
-        project(0, 1, 0)
-        project(0, 1, 1)
-        project(0, 1, 2)
-        project(0, 1, 3)
+        for n in range(4):
+            project(0, 1, n)
         quantize_v(0, 0)
         quantize_jac(1, 1)
         slopes(1, 1)
         similarities(2)
         quantize_v(0, 1)
         quantize_h(1)
+
         project(1, 0, 0)
         project(1, 0, 1)
-        interleave_jac(2, 0, 0, False)
+        interleave_jac(on_scalar, 2, 0, LOW)
         slopes(2, 0)
         forces(0, 0)
         project(1, 0, 2)
         forces(0, 1)
         slopes(2, 1)
-        interleave_jac(2, 0, 1, False)
+        interleave_jac(on_scalar, 2, 0, HIGH)
         project(1, 0, 3)
         forces(0, 2)
         quantize_h(2)
         project(1, 1, 0)
-        interleave_jac(2, 1, 0, False)
         forces(0, 3)
         quantize_v(1, 0)
         project(1, 1, 1)
-        quantize_jac(2, 0)
-        forces(0, 4)
+        interleave_jac(on_scalar, 2, 1, LOW)
         project(1, 1, 2)
-        interleave_jac(2, 1, 1, False)
-        forces(0, 5)
+        forces(0, 4)
+        interleave_jac(on_vector, 2, 1, HIGH)
+        quantize_jac(2, 0)
         project(1, 1, 3)
+        forces(0, 5)
+
         quantize_jac(2, 1)
-        similarity_bank(3, 0, 0)
-        similarity_bank(3, 0, 1)
         quantize_v(1, 1)
-        similarity_bank(3, 1, 0)
-        similarity_bank(3, 1, 1)
+        similarities(3)
         slopes(3, 0)
+
         project(2, 0, 0)
         forces(1, 0)
         slopes(3, 1)
@@ -347,13 +355,12 @@ def tile_cubic_kernel_forces_s12_kernel(
         forces(1, 6)
         forces(1, 7)
         project(3, 1, 1)
+
         forces(2, 0, 2)
         quantize_v(3, 1)
-        forces(2, 2, 2)
-        forces(2, 4, 2)
-        forces(2, 6, 2)
-        forces(3, 0, 2)
-        forces(3, 2, 2)
-        forces(3, 4, 2)
+        for mt in (2, 4, 6):
+            forces(2, mt, 2)
+        for mt in (0, 2, 4):
+            forces(3, mt, 2)
         forces(3, 6)
         forces(3, 7)

from contextlib import ExitStack

import concourse.mybir as mybir
from concourse.masks import make_identity

M, D, J, C = 1024, 1024, 1024, 1536
FLOPS = 2 * M * D * J + 2 * J * D * C + 2 * M * J * C

F32 = mybir.dt.float32
BF16 = mybir.dt.bfloat16
I32 = mybir.dt.int32
U32 = mybir.dt.uint32
U8 = mybir.dt.uint8
FP8X4 = mybir.dt.float8_e4m3fn_x4
FP4X4 = mybir.dt.float4_e2m1fn_x4
SQUARE = mybir.ActivationFunctionType.Square
MULT = mybir.AluOpType.mult
ADD = mybir.AluOpType.add

P = 128
SLOTS = 4
K_PASS = P * SLOTS
PASSES = 2
RUN = 8
BANK = 512
BANKS = 8
GROUP = 256
GROUPS = M // GROUP
JAC_COLS = 512
JAC_CHUNKS = C // JAC_COLS
V_PIECES = ((0, 512), (512, 512), (1024, 256), (1280, 256))
LOW, HIGH, WHOLE = slice(0, JAC_COLS // 2), slice(JAC_COLS // 2, JAC_COLS), slice(0, JAC_COLS)


def tile_cubic_kernel_forces_s12_kernel(
    tc, frames_words, frames_scales, refs_words, refs_scales, coef, xref, jac, base, out
):
    nc = tc.nc
    with ExitStack() as ctx:
        keep = ctx.enter_context(tc.tile_pool(name="keep", bufs=1))
        ring = ctx.enter_context(tc.tile_pool(name="ring", bufs=2))
        psum = ctx.enter_context(tc.psum_pool(name="psum", bufs=BANKS))
        ctx.enter_context(tc.manual_schedule())

        def kept(name, shape, dtype):
            return keep.tile(shape, dtype, name=name, align_bytes=64)

        def mx_pair(name, width):
            return kept(name + "_codes", [P, width], U32), kept(name + "_scales", [P, width], U8)

        def new_bank():
            return psum.tile([P, BANK], F32, name="bank")

        two = range(PASSES)
        refs_raw = kept("refs_raw", [P, PASSES, 2 * J], U8)
        refs_plane_raw = kept("refs_plane_raw", [P, PASSES, J], U8)
        frames_plane = kept("frames_plane", [P, PASSES, M], U8)
        frames = [kept("frames%d" % h, [P, PASSES, M], U8) for h in range(2)]
        refs = [kept("refs%d" % jg, [P, PASSES, 2 * K_PASS], U8) for jg in two]
        refs_plane = [kept("refs_plane%d" % jg, [P, PASSES, K_PASS], U8) for jg in two]
        coef_rows = kept("coef_rows", [SLOTS, PASSES * P], BF16)
        coef_wide = kept("coef_wide", [P, PASSES * P], F32)
        coef_slot = kept("coef_slot", [P, PASSES, SLOTS], F32)
        ident = kept("ident", [P, P], F32)
        base_rows = kept("base_rows", [P, C], BF16)
        xref_raw = {(jg, h): kept("xref_raw%d%d" % (jg, h), [P, 2, D], BF16) for jg in two for h in range(2)}
        jac_raw = {
            (cc, g): kept("jac_raw%d%d" % (cc, g), [P, SLOTS, JAC_COLS], BF16) for cc in range(JAC_CHUNKS) for g in two
        }

        xref_q = {(jg, g): mx_pair("xref_q%d%d" % (jg, g), K_PASS) for jg in two for g in two}
        jac_q = {(cc, g): mx_pair("jac_q%d%d" % (cc, g), JAC_COLS) for cc in range(JAC_CHUNKS) for g in two}
        v_q = {(vc, jg): mx_pair("v_q%d%d" % (vc, jg), V_PIECES[vc][1]) for vc in range(len(V_PIECES)) for jg in two}
        h_q = [mx_pair("h_q%d" % mg, PASSES * GROUP) for mg in range(GROUPS)]

        squares, h_bf, xref_bf, jac_bf, v_bf = {}, {}, {}, {}, {}

        def quantize(pair, src):
            codes, scales = pair
            nc.vector.quantize_mx(out=codes[:].bitcast(FP8X4), scales=scales[:], in_=src)

        def load_scale_rows(plane, scales):
            rows = scales.rearrange("g (a r) n -> r a g n", r=4)
            for r in range(4):
                nc.sync.dma_start(out=plane[:].bitcast(I32)[r:P:32], in_=rows[r].bitcast(I32))

        def load_frames(h):
            nc.sync.dma_start(
                out=frames[h][:].bitcast(I32),
                in_=frames_words.rearrange("g p b -> p g b")[:, :, h * M : (h + 1) * M].bitcast(I32),
            )

        def load_xref(queue, jg, h):
            r0 = jg * K_PASS + h * 2 * P
            queue.dma_start(out=xref_raw[jg, h][:], in_=xref[r0 : r0 + 2 * P, :].rearrange("(a p) d -> p a d", p=P))

        def load_jac(cc):
            for g in two:
                rows = jac[g * K_PASS : (g + 1) * K_PASS, cc * JAC_COLS : (cc + 1) * JAC_COLS]
                nc.sync.dma_start(out=jac_raw[cc, g][:], in_=rows.rearrange("(p t) c -> p t c", t=SLOTS))

        def sort_refs(jg):
            for dst, src, words in ((refs[jg], refs_raw, 4), (refs_plane[jg], refs_plane_raw, 2)):
                width = words * K_PASS // RUN
                part = src[:].bitcast(I32)[:, :, jg * width : (jg + 1) * width]
                nc.vector.tensor_copy(
                    out=dst[:].bitcast(I32).rearrange("p g (t q w) -> p g t q w", t=SLOTS, w=words),
                    in_=part.rearrange("p g (q t w) -> p g t q w", t=SLOTS, w=words),
                )

        def spread_coef():
            nc.vector.tensor_copy(out=coef_wide[0:SLOTS, :], in_=coef_rows[:])
            bank = new_bank()
            for jg in two:
                nc.tensor.transpose(bank[:, jg * P : (jg + 1) * P], coef_wide[:, jg * P : (jg + 1) * P], ident[:])
            turned = bank[:, 0 : PASSES * P].rearrange("p (g k) -> p g k", g=PASSES)
            nc.vector.tensor_copy(out=coef_slot[:], in_=turned[:, :, 0:SLOTS])

        def similarity_bank(mg, jg, pair):
            if jg == 0 and pair == 0:
                squares[mg] = ring.tile([P, PASSES, 2, GROUP, 2], F32, name="squares", align_bytes=64)
            b0 = (mg % 2) * 2 * GROUP
            bank = new_bank()
            for e in range(2):
                t = 2 * pair + e
                for g in two:
                    nc.tensor.matmul_mx(
                        out=bank[:, e * GROUP : (e + 1) * GROUP],
                        lhsT=refs[jg][:, g, t * 2 * P : (t + 1) * 2 * P].bitcast(FP4X4),
                        lhsT_scale=refs_plane[jg][:, g, t * P : (t + 1) * P],
                        rhs=frames[mg // 2][:, g, b0 : b0 + 2 * GROUP].bitcast(FP4X4),
                        rhs_scale=frames_plane[:, g, mg * GROUP : (mg + 1) * GROUP],
                        start=(g == 0),
                        stop=(g == PASSES - 1),
                    )
            nc.scalar.activation(
                out=squares[mg][:, jg, pair], in_=bank[:].rearrange("p (e n) -> p n e", e=2), func=SQUARE
            )

        def similarities(mg):
            for jg in two:
                for pair in range(2):
                    similarity_bank(mg, jg, pair)

        def slopes(mg, jg):
            if jg == 0:
                h_bf[mg] = ring.tile([P, PASSES, GROUP, SLOTS], BF16, name="h_bf", align_bytes=64)
            factor = coef_slot[:, jg].rearrange("p (a e) -> p a e", e=2).unsqueeze(1)
            nc.vector.tensor_tensor(
                out=h_bf[mg][:, jg].rearrange("p n (a e) -> p n a e", e=2),
                in0=squares[mg][:, jg].rearrange("p a n e -> p n a e"),
                in1=factor.to_broadcast([P, GROUP, 2, 2]),
                op=MULT,
            )

        def quantize_h(mg):
            quantize(h_q[mg], h_bf[mg][:].rearrange("p g n t -> p (g n t)"))

        def turn_xref(jg):
            for g in two:
                xref_bf[jg, g] = ring.tile([P, K_PASS * SLOTS], BF16, name="xref_bf", bufs=4, align_bytes=64)
            for h in range(2):
                words = xref_raw[jg, h][:].bitcast(F32)
                for g in two:
                    bank = new_bank()
                    w0 = g * K_PASS // 2
                    for u in range(2):
                        for a in range(2):
                            c0 = (2 * u + a) * P
                            nc.tensor.transpose(
                                bank[:, c0 : c0 + P], words[:, a, w0 + u : w0 + K_PASS // 2 : 2], ident[:]
                            )
                    dst = xref_bf[jg, g][:].bitcast(F32)
                    nc.scalar.copy(
                        out=dst.rearrange("p (t h q r u) -> p h t q r u", t=SLOTS, h=2, r=RUN, u=2)[:, h],
                        in_=bank[:].rearrange("p (u q t r) -> p t q r u", u=2, t=SLOTS, r=RUN),
                    )

        def quantize_xref(jg):
            for g in two:
                quantize(xref_q[jg, g], xref_bf[jg, g][:])

        def interleave_jac(copy, cc, g, cols):
            if (cc, g) not in jac_bf:
                jac_bf[cc, g] = ring.tile([P, JAC_COLS, SLOTS], BF16, name="jac_bf", bufs=3, align_bytes=64)
            copy(
                out=jac_bf[cc, g][:, cols, :].rearrange("p (c i) t -> p c t i", i=4),
                in_=jac_raw[cc, g][:, :, cols].rearrange("p t (c i) -> p c t i", i=4),
            )

        def quantize_jac(cc, g):
            quantize(jac_q[cc, g], jac_bf[cc, g][:].rearrange("p c t -> p (c t)"))

        def project(vc, jg, n):
            c0, width = V_PIECES[vc]
            if n == 0:
                v_bf[vc, jg] = ring.tile([P, width, SLOTS], BF16, name="v_bf", bufs=3, align_bytes=64)
            bank = new_bank()
            cc, first = divmod(c0 + n * P, JAC_COLS)
            cols = slice(first, first + P)
            for t in range(SLOTS):
                quarter = slice(t * P, (t + 1) * P)
                for g in two:
                    nc.tensor.matmul_mx(
                        out=bank[:, quarter],
                        lhsT=xref_q[jg, g][0][:, quarter].bitcast(FP8X4),
                        lhsT_scale=xref_q[jg, g][1][:, quarter],
                        rhs=jac_q[cc, g][0][:, cols].bitcast(FP8X4),
                        rhs_scale=jac_q[cc, g][1][:, cols],
                        start=(g == 0),
                        stop=(g == PASSES - 1),
                    )
            nc.scalar.copy(
                out=v_bf[vc, jg][:, n * P : (n + 1) * P, :], in_=bank[:].rearrange("p (t n) -> p n t", t=SLOTS)
            )

        def quantize_v(vc, jg):
            quantize(v_q[vc, jg], v_bf[vc, jg][:].rearrange("p c t -> p (c t)"))

        def forces(vc, mt, tiles=1):
            c0, width = V_PIECES[vc]
            bank = new_bank()
            codes, scales = h_q[mt // 2]
            for a in range(tiles):
                for jg in two:
                    m0 = jg * GROUP + (mt % 2 + a) * P
                    nc.tensor.matmul_mx(
                        out=bank[:, a * width : (a + 1) * width],
                        lhsT=codes[:, m0 : m0 + P].bitcast(FP8X4),
                        lhsT_scale=scales[:, m0 : m0 + P],
                        rhs=v_q[vc, jg][0][:].bitcast(FP8X4),
                        rhs_scale=v_q[vc, jg][1][:],
                        start=(jg == 0),
                        stop=(jg == PASSES - 1),
                    )
            res = ring.tile([P, tiles, width], F32, name="res", bufs=BANKS, align_bytes=64)
            nc.vector.tensor_tensor(
                out=res[:],
                in0=bank[:, 0 : tiles * width].rearrange("p (a c) -> p a c", a=tiles),
                in1=base_rows[:, c0 : c0 + width].unsqueeze(1).to_broadcast([P, tiles, width]),
                op=ADD,
            )
            rows = out[mt * P : (mt + tiles) * P, c0 : c0 + width]
            nc.sync.dma_start(out=rows.rearrange("(a p) c -> p a c", p=P), in_=res[:])

        on_vector, on_scalar = nc.vector.tensor_copy, nc.scalar.copy

        nc.gpsimd.memset(refs_plane_raw[:].bitcast(I32), 0)
        nc.gpsimd.memset(frames_plane[:].bitcast(I32), 0)
        nc.gpsimd.memset(coef_wide[:], 0.0)
        make_identity(nc, ident[:])

        nc.sync.dma_start(
            out=coef_rows[:].rearrange("t (a r) -> t a r", r=RUN),
            in_=coef.rearrange("(a t r) -> t a r", t=SLOTS, r=RUN),
        )
        load_scale_rows(refs_plane_raw, refs_scales)
        load_xref(nc.scalar, 0, 0)
        load_xref(nc.sync, 0, 1)
        nc.sync.dma_start(out=refs_raw[:].bitcast(I32), in_=refs_words.rearrange("g p b -> p g b").bitcast(I32))
        load_frames(0)
        load_scale_rows(frames_plane, frames_scales)
        load_jac(0)
        load_xref(nc.sync, 1, 0)
        load_xref(nc.sync, 1, 1)
        load_jac(1)
        load_frames(1)
        load_jac(2)
        nc.sync.dma_start(out=base_rows[:], in_=base.partition_broadcast(P))


        spread_coef()
        turn_xref(0)
        sort_refs(0)
        sort_refs(1)
        quantize_xref(0)

        interleave_jac(on_scalar, 0, 0, HIGH)
        similarities(0)
        similarities(1)
        interleave_jac(on_vector, 0, 0, LOW)
        interleave_jac(on_vector, 0, 1, WHOLE)
        quantize_jac(0, 0)
        slopes(0, 0)
        quantize_jac(0, 1)
        slopes(0, 1)
        slopes(1, 0)
        quantize_h(0)

        turn_xref(1)
        quantize_xref(1)
        for n in range(4):
            project(0, 0, n)
        interleave_jac(on_vector, 1, 0, WHOLE)
        interleave_jac(on_vector, 1, 1, WHOLE)
        quantize_jac(1, 0)
        for n in range(4):
            project(0, 1, n)
        quantize_v(0, 0)
        quantize_jac(1, 1)
        slopes(1, 1)
        similarities(2)
        quantize_v(0, 1)
        quantize_h(1)

        project(1, 0, 0)
        project(1, 0, 1)
        interleave_jac(on_scalar, 2, 0, LOW)
        slopes(2, 0)
        forces(0, 0)
        project(1, 0, 2)
        forces(0, 1)
        slopes(2, 1)
        interleave_jac(on_scalar, 2, 0, HIGH)
        project(1, 0, 3)
        forces(0, 2)
        quantize_h(2)
        project(1, 1, 0)
        forces(0, 3)
        quantize_v(1, 0)
        project(1, 1, 1)
        interleave_jac(on_scalar, 2, 1, LOW)
        project(1, 1, 2)
        forces(0, 4)
        interleave_jac(on_vector, 2, 1, HIGH)
        quantize_jac(2, 0)
        project(1, 1, 3)
        forces(0, 5)

        quantize_jac(2, 1)
        quantize_v(1, 1)
        similarities(3)
        slopes(3, 0)

        project(2, 0, 0)
        forces(1, 0)
        slopes(3, 1)
        project(2, 0, 1)
        forces(1, 1)
        project(2, 1, 0)
        quantize_v(2, 0)
        quantize_h(3)
        forces(1, 2)
        project(2, 1, 1)
        forces(1, 3)
        project(3, 0, 0)
        forces(1, 4)
        quantize_v(2, 1)
        forces(1, 5)
        project(3, 0, 1)
        forces(0, 6)
        forces(0, 7)
        quantize_v(3, 0)
        project(3, 1, 0)
        forces(1, 6)
        forces(1, 7)
        project(3, 1, 1)

        forces(2, 0, 2)
        quantize_v(3, 1)
        for mt in (2, 4, 6):
            forces(2, mt, 2)
        for mt in (0, 2, 4):
            forces(3, mt, 2)
        forces(3, 6)
        forces(3, 7)
